import numpy as np
import ml_dtypes


def mxq(x, axis, fmt="e4m3"):
    dtype, down = {"e4m3": (ml_dtypes.float8_e4m3fn, 7), "e5m2": (ml_dtypes.float8_e5m2, 14)}[fmt]
    v = np.moveaxis(np.asarray(x, np.float32).astype(ml_dtypes.bfloat16).astype(np.float64), axis, -1)
    blocks = v.reshape(v.shape[:-1] + (-1, 32))
    amax = np.abs(blocks).max(-1, keepdims=True)
    byte = np.maximum(np.where(amax > 0, np.frexp(amax)[1] - 1 + 127, 0) - down, 1)
    scale = np.exp2(byte - 127.0)
    codes = (blocks / scale).astype(np.float32).astype(dtype).astype(np.float64)
    return np.moveaxis((codes * scale).reshape(v.shape), -1, axis)


WIDE = False


def mx_kscale(k):
    if not WIDE:
        return np.ones(k)
    levels = np.array([10, -10, 5, -5, 0])
    if k % 512:
        return np.exp2(np.random.permutation(np.resize(levels, k // 32))).repeat(32)
    a = np.empty((k // 512, 16))
    for p in range(k // 512):
        a[p, :8] = np.random.permutation(np.resize(levels, 8))
        for g in range(8):
            far = levels[np.abs(levels - a[p, g]) >= 10]
            a[p, g + 8] = far[np.random.randint(len(far))]
    return np.exp2(a.ravel()).repeat(32)


def f64(x):
    return np.asarray(x).astype(np.float64)


E2M1 = np.array([0.0, 0.5, 1.0, 1.5, 2.0, 3.0, 4.0, 6.0, -0.0, -0.5, -1.0, -1.5, -2.0, -3.0, -4.0, -6.0])


def pack_weight(w, fmt):
    k, n = w.shape
    w = f64(np.asarray(w, np.float32).astype(ml_dtypes.bfloat16)).reshape(k // 32, 32, n)
    amax = np.abs(w).max(1)
    if fmt == "e4m3":
        byte = np.frexp(amax)[1] - 1 + 127 - 7
    else:
        mant, ex = np.frexp(amax / 6.0)
        byte = np.where(mant > 0.5, ex, ex - 1) + 127
    byte = np.clip(np.where(amax > 0, byte, 1), 1, 254)
    scaled = (w * np.exp2(127.0 - byte)[:, None, :]).reshape(k, n).astype(np.float32)
    by_word = np.ascontiguousarray(scaled.reshape(k // 512, 128, 4, n).transpose(0, 1, 3, 2))
    if fmt == "e4m3":
        words = by_word.astype(ml_dtypes.float8_e4m3fn).view(np.uint8)
    else:
        c = by_word.astype(ml_dtypes.float4_e2m1fn).view(np.uint8) & 0xF
        words = (c[..., 0::2] | (c[..., 1::2] << 4)).reshape(k // 512, 128, 2 * n)
    return np.ascontiguousarray(words), np.ascontiguousarray(byte.astype(np.uint8).reshape(k // 512, 16, n))


def unpack_weight(words, scales, fmt):
    g, _, n = scales.shape
    words = np.ascontiguousarray(words).reshape(g, 128, n, -1)
    if fmt == "e4m3":
        vals = words.view(ml_dtypes.float8_e4m3fn).astype(np.float64)
    else:
        nib = np.empty((g, 128, n, 4), np.uint8)
        nib[..., 0::2] = words & 0xF
        nib[..., 1::2] = words >> 4
        vals = E2M1[nib]
    vals = vals * np.repeat(np.exp2(scales.astype(np.float64) - 127.0), 8, axis=1)[..., None]
    return vals.transpose(0, 1, 3, 2).reshape(g * 512, n)


def planes(y):
    n, m = y.shape
    v = y.astype(np.float32).astype(ml_dtypes.bfloat16).astype(np.float64).reshape(n // 32, 32, m)
    top = np.abs(v).max(1)
    byte = np.clip(np.where(top > 0, np.frexp(top)[1] - 1 + 127 - 7, 1), 1, 254)
    codes = (v * np.exp2(127.0 - byte)[:, None, :]).reshape(n, m).astype(np.float32).astype(ml_dtypes.float8_e4m3fn).view(np.uint8)
    words = codes.reshape(n // 512, 128, 4, m).transpose(0, 1, 3, 2)
    return np.ascontiguousarray(words), np.ascontiguousarray(byte.astype(np.uint8).reshape(n // 512, 16, m))


O, K, M, T = 512, 3072, 512, 1024


def setup_inputs():
    n = np.random.standard_normal
    s = mx_kscale(K)[:, None]
    x = n((K, T)); x[:O] *= 6.0
    w = n((K, M)) / np.sqrt(K) / s; w[:O] /= 2.0
    p_x4 = pack_weight(x[O:] * s[O:], "e2m1")
    p_w4 = pack_weight(w[O:], "e2m1")
    return {
        "x8": (x[:O] * s[:O]).astype(np.float32),
        "w8": (w[:O]).astype(np.float32),
        "x4_words": p_x4[0],
        "x4_scales": p_x4[1],
        "w4_words": p_w4[0],
        "w4_scales": p_w4[1],
        "g": (n((1024, 512))).astype(np.float32),
    }


def reference(x8, w8, x4_words, x4_scales, w4_words, w4_scales, g):
    x8_ = mxq(f64(x8), 0, "e4m3")
    w8_ = mxq(f64(w8), 0, "e4m3")
    x4_ = unpack_weight(x4_words, x4_scales, "e2m1")
    w4_ = unpack_weight(w4_words, w4_scales, "e2m1")
    y = x8_.T @ w8_ + x4_.T @ w4_
    out_0 = f64(g) * y
    return (out_0,) + planes(out_0)

@@ -1,0 +1,272 @@
+from contextlib import ExitStack
+
+import concourse.mybir as mybir
+
+O, K4, N, T = 512, 2560, 512, 1024
+FLOPS = 2 * T * N * (O + K4)
+
+F32 = mybir.dt.float32
+BF16 = mybir.dt.bfloat16
+I32 = mybir.dt.int32
+U32 = mybir.dt.uint32
+U16 = mybir.dt.uint16
+U8 = mybir.dt.uint8
+FP8X4 = mybir.dt.float8_e4m3fn_x4
+FP4X4 = mybir.dt.float4_e2m1fn_x4
+
+P = 128
+PACK = 4
+PASSES = K4 // (P * PACK)
+HALF = P * PACK
+NH = N // 2
+V_COLS = 160
+
+
+def tile_mix_atom_tm_pl_mul_kernel(
+    tc, x8, w8, x4_words, x4_scales, w4_words, w4_scales, g, out_0, out_1, out_2
+):
+    nc = tc.nc
+    with ExitStack() as ctx:
+        sb = ctx.enter_context(tc.tile_pool(name="sb", bufs=1))
+        psum = ctx.enter_context(tc.psum_pool(name="psum", bufs=1))
+        ctx.enter_context(tc.manual_schedule())
+
+        def tile(name, shape, dtype):
+            return sb.tile(shape, dtype, name=name, align_bytes=64)
+
+        x4_i32 = x4_words.bitcast(I32).rearrange("a p c -> p a c")
+        w4_i32 = w4_words.bitcast(I32).rearrange("a p c -> p a c")
+        xs_rows = x4_scales.bitcast(I32).rearrange("a (q r) c -> r q a c", r=PACK)
+        ws_rows = w4_scales.bitcast(I32).rearrange("a (q r) c -> r q a c", r=PACK)
+        os_rows = out_2.bitcast(I32).rearrange("a (q r) c -> r q a c", r=PACK)
+        ow_i32 = out_1.rearrange("a p n i -> a p (n i)").bitcast(I32)
+
+        w4_sb = {}
+        x4_raw = {}
+
+        def load_w4(a0, a1):
+            t = tile("w4_%d" % a0, [P, (a1 - a0) * 2 * N], U8)
+            nc.sync.dma_start(
+                out=t[:].bitcast(I32).rearrange("p (a c) -> p a c", a=a1 - a0), in_=w4_i32[:, a0:a1, :]
+            )
+            for a in range(a0, a1):
+                w4_sb[a] = t[:, (a - a0) * 2 * N : (a - a0 + 1) * 2 * N]
+
+        def load_x4(a0, a1, h0, h1):
+            width = (h1 - h0) * 2 * HALF
+            t = tile("x4_%d_%d" % (a0, h0), [P, (a1 - a0) * width], U8)
+            nc.sync.dma_start(
+                out=t[:].bitcast(I32).rearrange("p (a c) -> p a c", a=a1 - a0),
+                in_=x4_i32[:, a0:a1, h0 * HALF // 2 : h1 * HALF // 2],
+            )
+            for a in range(a0, a1):
+                for h in range(h0, h1):
+                    c0 = (a - a0) * width + (h - h0) * 2 * HALF
+                    x4_raw[h, a] = t[:, c0 : c0 + 2 * HALF]
+
+        def load_scale_rows(plane, rows):
+            for r in range(PACK):
+                nc.sync.dma_start(
+                    out=plane[r:P:32, :].bitcast(I32).rearrange("q (a c) -> q a c", a=PASSES), in_=rows[r]
+                )
+
+        def load_rows(name, src):
+            t = tile(name, [P, src.shape[1], src.shape[2]], F32)
+            nc.sync.dma_start(out=t[:], in_=src)
+            return t
+
+        ws_plane = tile("ws_plane", [P, PASSES * N], U8)
+        xs_raw = tile("xs_raw", [P, PASSES * T], U8)
+        nc.vector.memset(ws_plane[:].bitcast(I32), 0)
+        nc.vector.memset(xs_raw[:].bitcast(I32), 0)
+
+        x8_rows = x8.rearrange("(p j) t -> p j t", j=PACK)
+        g_rows = g.rearrange("(h p r) n -> h p r n", p=P, r=PACK)
+        o_rows = out_0.rearrange("(h p r) n -> h p r n", p=P, r=PACK)
+
+        load_w4(0, 1)
+        load_x4(0, 1, 0, 1)
+        load_scale_rows(ws_plane, ws_rows)
+        load_scale_rows(xs_raw, xs_rows)
+        load_w4(1, 3)
+        load_x4(1, 3, 0, 1)
+        load_w4(3, 5)
+        load_x4(3, 5, 0, 2)
+        w8_raw = load_rows("w8_raw", w8.rearrange("(p j) n -> p j n", j=PACK))
+        x8_raw = {0: load_rows("x8_raw0", x8_rows[:, :, :HALF])}
+        load_x4(0, 3, 1, 2)
+        g_sb = {}
+        for rp in range(2):
+            g_sb[0, rp] = load_rows("g0_%d" % rp, g_rows[0, :, 2 * rp : 2 * rp + 2, :])
+        x8_raw[1] = load_rows("x8_raw1", x8_rows[:, :, HALF:])
+        for rp in range(2):
+            g_sb[1, rp] = load_rows("g1_%d" % rp, g_rows[1, :, 2 * rp : 2 * rp + 2, :])
+
+        x4_dealt = {}
+        xs_dealt = {}
+
+        def deal_words(h, a):
+            t = tile("x4d_%d_%d" % (h, a), [P, 2 * HALF], U8)
+            nc.scalar.copy(
+                out=t[:].bitcast(U16).rearrange("p (r m) -> p r m", r=PACK),
+                in_=x4_raw[h, a].bitcast(U16).rearrange("p (m r) -> p r m", r=PACK),
+            )
+            x4_dealt[h, a] = t
+
+        def deal_scales(h, a0, a1):
+            t = tile("xsd_%d_%d" % (h, a0), [P, (a1 - a0) * HALF], U8)
+            src = xs_raw[:].rearrange("p (a h m r) -> p h r a m", a=PASSES, h=2, r=PACK)
+            nc.vector.tensor_copy(
+                out=t[:].rearrange("p (a r m) -> p r a m", r=PACK, m=P), in_=src[:, h, :, a0:a1, :]
+            )
+            for a in range(a0, a1):
+                xs_dealt[h, a] = t[:, (a - a0) * HALF : (a - a0 + 1) * HALF]
+
+        acc = {}
+        for h in range(2):
+            for r in range(PACK):
+                acc[h, r] = psum.tile([P, N], F32, name="acc_%d_%d" % (h, r))
+        opened = set()
+
+        def fp4_pass(h, a):
+            for r in range(PACK):
+                nc.tensor.matmul_mx(
+                    out=acc[h, r][:],
+                    lhsT=x4_dealt[h, a][:, 2 * P * r : 2 * P * (r + 1)].bitcast(FP4X4),
+                    lhsT_scale=xs_dealt[h, a][:, P * r : P * (r + 1)],
+                    rhs=w4_sb[a].bitcast(FP4X4),
+                    rhs_scale=ws_plane[:, a * N : (a + 1) * N],
+                    start=h not in opened,
+                    stop=False,
+                )
+            opened.add(h)
+
+        w8_codes = tile("w8_codes", [P, N], U32)
+        w8_plane = tile("w8_plane", [P, N], U8)
+        x8_bf = {}
+        x8_codes = {}
+        x8_plane = {}
+
+        def round_x8(copy, h, rp):
+            t = tile("x8_bf_%d_%d" % (h, rp), [P, 2 * P * PACK], BF16)
+            src = x8_raw[h][:].rearrange("p j (m r) -> p m r j", r=PACK)
+            copy(
+                out=t[:].rearrange("p (r m j) -> p m r j", r=2, j=PACK),
+                in_=src[:, :, 2 * rp : 2 * rp + 2, :],
+            )
+            x8_bf[h, rp] = t
+
+        def quantize_x8(h, rp):
+            codes = tile("x8_codes_%d_%d" % (h, rp), [P, 2 * P], U32)
+            plane = tile("x8_plane_%d_%d" % (h, rp), [P, 2 * P], U8)
+            nc.vector.quantize_mx(out=codes[:].bitcast(FP8X4), scales=plane[:], in_=x8_bf[h, rp][:])
+            x8_codes[h, rp] = codes
+            x8_plane[h, rp] = plane
+
+        def fp8_pass(h):
+            for r in range(PACK):
+                cols = slice(P * (r % 2), P * (r % 2 + 1))
+                nc.tensor.matmul_mx(
+                    out=acc[h, r][:],
+                    lhsT=x8_codes[h, r // 2][:, cols].bitcast(FP8X4),
+                    lhsT_scale=x8_plane[h, r // 2][:, cols],
+                    rhs=w8_codes[:].bitcast(FP8X4),
+                    rhs_scale=w8_plane[:],
+                    start=False,
+                    stop=True,
+                )
+
+        res = {h: tile("res_%d" % h, [P, PACK, N], F32) for h in range(2)}
+        res_bf = {(h, nh): tile("res_bf_%d_%d" % (h, nh), [P, NH * PACK], BF16) for h in range(2) for nh in range(2)}
+        o_codes = {h: tile("o_codes_%d" % h, [P, N], U32) for h in range(2)}
+        o_plane = tile("o_plane", [P, 2 * N], U8)
+
+        def gate(h, nh):
+            cols = slice(nh * NH, (nh + 1) * NH)
+            for r in range(PACK):
+                nc.vector.tensor_tensor(
+                    out=res[h][:, r, cols],
+                    in0=acc[h, r][:, cols],
+                    in1=g_sb[h, r // 2][:, r % 2, cols],
+                    op=mybir.AluOpType.mult,
+                )
+
+        def round_result(copy, h, nh, c0, c1):
+            src = res[h][:, :, nh * NH + c0 : nh * NH + c1]
+            dst = res_bf[h, nh][:, PACK * c0 : PACK * c1]
+            copy(
+                out=dst.rearrange("p (c i r) -> p c r i", i=4, r=PACK),
+                in_=src.rearrange("p r (c i) -> p c r i", i=4),
+            )
+
+        def quantize_result(h, nh):
+            nc.vector.quantize_mx(
+                out=o_codes[h][:, nh * NH : (nh + 1) * NH].bitcast(FP8X4),
+                scales=o_plane[:, h * N + nh * NH : h * N + (nh + 1) * NH],
+                in_=res_bf[h, nh][:],
+            )
+
+        def store_codes(h, c0, c1):
+            nc.sync.dma_start(out=ow_i32[h, :, c0:c1], in_=o_codes[h][:, c0:c1].bitcast(I32))
+
+        deal_words(0, 0)
+        deal_scales(0, 0, 1)
+        fp4_pass(0, 0)
+        deal_scales(0, 1, PASSES)
+        for a in range(1, PASSES):
+            deal_words(0, a)
+            fp4_pass(0, a)
+        deal_scales(1, 3, 5)
+        deal_scales(1, 0, 3)
+        deal_words(1, 3)
+        deal_words(1, 4)
+
+        w8_bf = tile("w8_bf", [P, N * PACK], BF16)
+        nc.vector.tensor_copy(
+            out=w8_bf[:].rearrange("p (c i j) -> p c j i", i=4, j=PACK),
+            in_=w8_raw[:].rearrange("p j (c i) -> p c j i", i=4),
+        )
+        nc.vector.quantize_mx(out=w8_codes[:].bitcast(FP8X4), scales=w8_plane[:], in_=w8_bf[:])
+
+        round_x8(nc.vector.tensor_copy, 0, 0)
+        round_x8(nc.scalar.copy, 0, 1)
+        quantize_x8(0, 0)
+        quantize_x8(0, 1)
+        fp4_pass(1, 3)
+        fp8_pass(0)
+        fp4_pass(1, 4)
+        for a in range(3):
+            deal_words(1, a)
+            fp4_pass(1, a)
+
+        gate(0, 0)
+        round_result(nc.scalar.copy, 0, 0, 0, NH)
+        gate(0, 1)
+        nc.sync.dma_start(out=o_rows[0], in_=res[0][:])
+
+        round_x8(nc.vector.tensor_copy, 1, 0)
+        round_x8(nc.scalar.copy, 1, 1)
+        quantize_result(0, 0)
+        quantize_x8(1, 0)
+        quantize_x8(1, 1)
+        fp8_pass(1)
+        round_result(nc.scalar.copy, 0, 1, 0, NH)
+
+        gate(1, 0)
+        round_result(nc.scalar.copy, 1, 0, 0, NH)
+        quantize_result(0, 1)
+        store_codes(0, 0, N)
+        gate(1, 1)
+        for rp in range(2):
+            nc.sync.dma_start(out=o_rows[1, :, 2 * rp : 2 * rp + 2, :], in_=res[1][:, 2 * rp : 2 * rp + 2, :])
+        round_result(nc.scalar.copy, 1, 1, V_COLS, NH)
+        round_result(nc.vector.tensor_copy, 1, 1, 0, V_COLS)
+        quantize_result(1, 0)
+        store_codes(1, 0, NH)
+        quantize_result(1, 1)
+        store_codes(1, NH, N)
+        for r in range(PACK):
+            queue = nc.sync if r % 2 else nc.scalar
+            queue.dma_start(
+                out=os_rows[r], in_=o_plane[r:P:32, :].bitcast(I32).rearrange("q (a c) -> q a c", a=2)
+            )

@@ -19,7 +19,6 @@ PACK = 4
 PASSES = K4 // (P * PACK)
 HALF = P * PACK
 NH = N // 2
-V_COLS = 160
 
 
 def tile_mix_atom_tm_pl_mul_kernel(
@@ -77,30 +76,40 @@ def tile_mix_atom_tm_pl_mul_kernel(
 
         ws_plane = tile("ws_plane", [P, PASSES * N], U8)
         xs_raw = tile("xs_raw", [P, PASSES * T], U8)
-        nc.vector.memset(ws_plane[:].bitcast(I32), 0)
         nc.vector.memset(xs_raw[:].bitcast(I32), 0)
+        nc.vector.memset(ws_plane[:].bitcast(I32), 0)
 
         x8_rows = x8.rearrange("(p j) t -> p j t", j=PACK)
         g_rows = g.rearrange("(h p r) n -> h p r n", p=P, r=PACK)
         o_rows = out_0.rearrange("(h p r) n -> h p r n", p=P, r=PACK)
 
+        x8_raw = {}
+        g_sb = {}
+
+        def load_x8(h0, h1):
+            t = load_rows("x8_raw%d" % h0, x8_rows[:, :, h0 * HALF : h1 * HALF])
+            for h in range(h0, h1):
+                x8_raw[h] = t[:, :, (h - h0) * HALF : (h - h0 + 1) * HALF]
+
+        def load_g(h, r0, r1):
+            t = load_rows("g%d_%d" % (h, r0), g_rows[h, :, r0:r1, :])
+            for r in range(r0, r1):
+                g_sb[h, r] = t[:, r - r0, :]
+
         load_w4(0, 1)
-        load_x4(0, 1, 0, 1)
-        load_scale_rows(ws_plane, ws_rows)
+        load_x4(0, 1, 0, 2)
         load_scale_rows(xs_raw, xs_rows)
+        load_scale_rows(ws_plane, ws_rows)
         load_w4(1, 3)
-        load_x4(1, 3, 0, 1)
+        load_x4(1, 3, 0, 2)
         load_w4(3, 5)
         load_x4(3, 5, 0, 2)
         w8_raw = load_rows("w8_raw", w8.rearrange("(p j) n -> p j n", j=PACK))
-        x8_raw = {0: load_rows("x8_raw0", x8_rows[:, :, :HALF])}
-        load_x4(0, 3, 1, 2)
-        g_sb = {}
-        for rp in range(2):
-            g_sb[0, rp] = load_rows("g0_%d" % rp, g_rows[0, :, 2 * rp : 2 * rp + 2, :])
-        x8_raw[1] = load_rows("x8_raw1", x8_rows[:, :, HALF:])
-        for rp in range(2):
-            g_sb[1, rp] = load_rows("g1_%d" % rp, g_rows[1, :, 2 * rp : 2 * rp + 2, :])
+        load_x8(0, 1)
+        load_g(0, 0, 4)
+        load_x8(1, 2)
+        load_g(1, 0, 2)
+        load_g(1, 2, 4)
 
         x4_dealt = {}
         xs_dealt = {}
@@ -128,18 +137,18 @@ def tile_mix_atom_tm_pl_mul_kernel(
                 acc[h, r] = psum.tile([P, N], F32, name="acc_%d_%d" % (h, r))
         opened = set()
 
-        def fp4_pass(h, a):
-            for r in range(PACK):
+        def fp4_pass(h, a, rows=range(PACK)):
+            for r in rows:
                 nc.tensor.matmul_mx(
                     out=acc[h, r][:],
                     lhsT=x4_dealt[h, a][:, 2 * P * r : 2 * P * (r + 1)].bitcast(FP4X4),
                     lhsT_scale=xs_dealt[h, a][:, P * r : P * (r + 1)],
                     rhs=w4_sb[a].bitcast(FP4X4),
                     rhs_scale=ws_plane[:, a * N : (a + 1) * N],
-                    start=h not in opened,
+                    start=(h, r) not in opened,
                     stop=False,
                 )
-            opened.add(h)
+                opened.add((h, r))
 
         w8_codes = tile("w8_codes", [P, N], U32)
         w8_plane = tile("w8_plane", [P, N], U8)
@@ -149,7 +158,7 @@ def tile_mix_atom_tm_pl_mul_kernel(
 
         def round_x8(copy, h, rp):
             t = tile("x8_bf_%d_%d" % (h, rp), [P, 2 * P * PACK], BF16)
-            src = x8_raw[h][:].rearrange("p j (m r) -> p m r j", r=PACK)
+            src = x8_raw[h].rearrange("p j (m r) -> p m r j", r=PACK)
             copy(
                 out=t[:].rearrange("p (r m j) -> p m r j", r=2, j=PACK),
                 in_=src[:, :, 2 * rp : 2 * rp + 2, :],
@@ -163,8 +172,8 @@ def tile_mix_atom_tm_pl_mul_kernel(
             x8_codes[h, rp] = codes
             x8_plane[h, rp] = plane
 
-        def fp8_pass(h):
-            for r in range(PACK):
+        def fp8_pass(h, rows=range(PACK)):
+            for r in rows:
                 cols = slice(P * (r % 2), P * (r % 2 + 1))
                 nc.tensor.matmul_mx(
                     out=acc[h, r][:],
@@ -181,13 +190,13 @@ def tile_mix_atom_tm_pl_mul_kernel(
         o_codes = {h: tile("o_codes_%d" % h, [P, N], U32) for h in range(2)}
         o_plane = tile("o_plane", [P, 2 * N], U8)
 
-        def gate(h, nh):
-            cols = slice(nh * NH, (nh + 1) * NH)
-            for r in range(PACK):
+        def gate(h, rows, c0, c1):
+            cols = slice(c0, c1)
+            for r in rows:
                 nc.vector.tensor_tensor(
                     out=res[h][:, r, cols],
                     in0=acc[h, r][:, cols],
-                    in1=g_sb[h, r // 2][:, r % 2, cols],
+                    in1=g_sb[h, r][:, cols],
                     op=mybir.AluOpType.mult,
                 )
 
@@ -209,64 +218,78 @@ def tile_mix_atom_tm_pl_mul_kernel(
         def store_codes(h, c0, c1):
             nc.sync.dma_start(out=ow_i32[h, :, c0:c1], in_=o_codes[h][:, c0:c1].bitcast(I32))
 
+        def store_rows(h, r0, r1):
+            nc.sync.dma_start(out=o_rows[h, :, r0:r1, :], in_=res[h][:, r0:r1, :])
+
+        def store_scales(queue):
+            for r in range(PACK):
+                queue.dma_start(
+                    out=os_rows[r], in_=o_plane[r:P:32, :].bitcast(I32).rearrange("q (a c) -> q a c", a=2)
+                )
+
+        w8_bf = tile("w8_bf", [P, N * PACK], BF16)
+
+        def round_w8(copy, c0, c1):
+            copy(
+                out=w8_bf[:, PACK * c0 : PACK * c1].rearrange("p (c i j) -> p c j i", i=4, j=PACK),
+                in_=w8_raw[:, :, c0:c1].rearrange("p j (c i) -> p c j i", i=4),
+            )
+
+        def quantize_w8():
+            nc.vector.quantize_mx(out=w8_codes[:].bitcast(FP8X4), scales=w8_plane[:], in_=w8_bf[:])
+
+        V = nc.vector.tensor_copy
+        S = nc.scalar.copy
+
         deal_words(0, 0)
         deal_scales(0, 0, 1)
         fp4_pass(0, 0)
+        deal_words(1, 0)
+        deal_scales(1, 0, 1)
+        fp4_pass(1, 0)
         deal_scales(0, 1, PASSES)
         for a in range(1, PASSES):
             deal_words(0, a)
             fp4_pass(0, a)
-        deal_scales(1, 3, 5)
-        deal_scales(1, 0, 3)
-        deal_words(1, 3)
-        deal_words(1, 4)
-
-        w8_bf = tile("w8_bf", [P, N * PACK], BF16)
-        nc.vector.tensor_copy(
-            out=w8_bf[:].rearrange("p (c i j) -> p c j i", i=4, j=PACK),
-            in_=w8_raw[:].rearrange("p j (c i) -> p c j i", i=4),
-        )
-        nc.vector.quantize_mx(out=w8_codes[:].bitcast(FP8X4), scales=w8_plane[:], in_=w8_bf[:])
-
-        round_x8(nc.vector.tensor_copy, 0, 0)
-        round_x8(nc.scalar.copy, 0, 1)
+        deal_scales(1, 1, PASSES)
+        for a in range(1, PASSES):
+            deal_words(1, a)
+        round_w8(V, 0, N)
+        quantize_w8()
+        round_x8(V, 0, 0)
+        round_x8(S, 0, 1)
         quantize_x8(0, 0)
         quantize_x8(0, 1)
-        fp4_pass(1, 3)
-        fp8_pass(0)
-        fp4_pass(1, 4)
-        for a in range(3):
-            deal_words(1, a)
+        for a in range(1, 2):
             fp4_pass(1, a)
-
-        gate(0, 0)
-        round_result(nc.scalar.copy, 0, 0, 0, NH)
-        gate(0, 1)
-        nc.sync.dma_start(out=o_rows[0], in_=res[0][:])
-
-        round_x8(nc.vector.tensor_copy, 1, 0)
-        round_x8(nc.scalar.copy, 1, 1)
+        fp8_pass(0)
+        for a in range(2, 4):
+            fp4_pass(1, a)
+        fp4_pass(1, 4, range(2))
+        gate(0, range(PACK), 0, NH)
+        round_result(S, 0, 0, 0, NH)
+        gate(0, range(PACK), NH, N)
+        store_rows(0, 0, 4)
+        round_x8(V, 1, 0)
+        round_x8(S, 1, 1)
         quantize_result(0, 0)
+        store_codes(0, 0, NH)
         quantize_x8(1, 0)
         quantize_x8(1, 1)
-        fp8_pass(1)
-        round_result(nc.scalar.copy, 0, 1, 0, NH)
-
-        gate(1, 0)
-        round_result(nc.scalar.copy, 1, 0, 0, NH)
+        fp8_pass(1, range(2))
+        fp4_pass(1, 4, range(2, PACK))
+        fp8_pass(1, range(2, PACK))
+        round_result(S, 0, 1, 0, NH)
+        gate(1, range(2), 0, N)
+        store_rows(1, 0, 2)
+        gate(1, range(2, PACK), 0, NH)
+        round_result(S, 1, 0, 0, NH)
+        gate(1, range(2, PACK), NH, N)
+        store_rows(1, 2, 4)
         quantize_result(0, 1)
-        store_codes(0, 0, N)
-        gate(1, 1)
-        for rp in range(2):
-            nc.sync.dma_start(out=o_rows[1, :, 2 * rp : 2 * rp + 2, :], in_=res[1][:, 2 * rp : 2 * rp + 2, :])
-        round_result(nc.scalar.copy, 1, 1, V_COLS, NH)
-        round_result(nc.vector.tensor_copy, 1, 1, 0, V_COLS)
+        store_codes(0, NH, N)
+        round_result(V, 1, 1, 0, NH)
         quantize_result(1, 0)
-        store_codes(1, 0, NH)
         quantize_result(1, 1)
-        store_codes(1, NH, N)
-        for r in range(PACK):
-            queue = nc.sync if r % 2 else nc.scalar
-            queue.dma_start(
-                out=os_rows[r], in_=o_plane[r:P:32, :].bitcast(I32).rearrange("q (a c) -> q a c", a=2)
-            )
+        store_codes(1, 0, N)
+        store_scales(nc.scalar)

@@ -106,8 +106,9 @@ def tile_mix_atom_tm_pl_mul_kernel(
         load_x4(3, 5, 0, 2)
         w8_raw = load_rows("w8_raw", w8.rearrange("(p j) n -> p j n", j=PACK))
         load_x8(0, 1)
-        load_g(0, 0, 4)
+        load_g(0, 0, 2)
         load_x8(1, 2)
+        load_g(0, 2, 4)
         load_g(1, 0, 2)
         load_g(1, 2, 4)
 
@@ -156,14 +157,14 @@ def tile_mix_atom_tm_pl_mul_kernel(
         x8_codes = {}
         x8_plane = {}
 
-        def round_x8(copy, h, rp):
-            t = tile("x8_bf_%d_%d" % (h, rp), [P, 2 * P * PACK], BF16)
-            src = x8_raw[h].rearrange("p j (m r) -> p m r j", r=PACK)
-            copy(
-                out=t[:].rearrange("p (r m j) -> p m r j", r=2, j=PACK),
-                in_=src[:, :, 2 * rp : 2 * rp + 2, :],
-            )
-            x8_bf[h, rp] = t
+        for h in range(2):
+            for rp in range(2):
+                x8_bf[h, rp] = tile("x8_bf_%d_%d" % (h, rp), [P, 2 * P * PACK], BF16)
+
+        def round_x8(copy, h, rp, m0=0, m1=P):
+            src = x8_raw[h].rearrange("p j (m r) -> p m j r", r=PACK)
+            dst = x8_bf[h, rp][:].rearrange("p (r m j) -> p m j r", r=2, j=PACK)
+            copy(out=dst[:, m0:m1], in_=src[:, m0:m1, :, 2 * rp : 2 * rp + 2])
 
         def quantize_x8(h, rp):
             codes = tile("x8_codes_%d_%d" % (h, rp), [P, 2 * P], U32)
@@ -221,10 +222,11 @@ def tile_mix_atom_tm_pl_mul_kernel(
         def store_rows(h, r0, r1):
             nc.sync.dma_start(out=o_rows[h, :, r0:r1, :], in_=res[h][:, r0:r1, :])
 
-        def store_scales(queue):
+        def store_scales(queue, h0=0, h1=2):
             for r in range(PACK):
                 queue.dma_start(
-                    out=os_rows[r], in_=o_plane[r:P:32, :].bitcast(I32).rearrange("q (a c) -> q a c", a=2)
+                    out=os_rows[r, :, h0:h1, :],
+                    in_=o_plane[r:P:32, h0 * N : h1 * N].bitcast(I32).rearrange("q (a c) -> q a c", a=h1 - h0),
                 )
 
         w8_bf = tile("w8_bf", [P, N * PACK], BF16)
@@ -266,19 +268,20 @@ def tile_mix_atom_tm_pl_mul_kernel(
         for a in range(2, 4):
             fp4_pass(1, a)
         fp4_pass(1, 4, range(2))
-        gate(0, range(PACK), 0, NH)
-        round_result(S, 0, 0, 0, NH)
-        gate(0, range(PACK), NH, N)
-        store_rows(0, 0, 4)
+
+        gate(0, range(2), 0, N)
+        store_rows(0, 0, 2)
         round_x8(V, 1, 0)
         round_x8(S, 1, 1)
-        quantize_result(0, 0)
-        store_codes(0, 0, NH)
         quantize_x8(1, 0)
-        quantize_x8(1, 1)
         fp8_pass(1, range(2))
         fp4_pass(1, 4, range(2, PACK))
+        gate(0, range(2, PACK), 0, NH)
+        round_result(S, 0, 0, 0, NH)
+        quantize_x8(1, 1)
         fp8_pass(1, range(2, PACK))
+        gate(0, range(2, PACK), NH, N)
+        store_rows(0, 2, 4)
         round_result(S, 0, 1, 0, NH)
         gate(1, range(2), 0, N)
         store_rows(1, 0, 2)
@@ -286,10 +289,12 @@ def tile_mix_atom_tm_pl_mul_kernel(
         round_result(S, 1, 0, 0, NH)
         gate(1, range(2, PACK), NH, N)
         store_rows(1, 2, 4)
+        quantize_result(0, 0)
         quantize_result(0, 1)
-        store_codes(0, NH, N)
+        store_codes(0, 0, N)
         round_result(V, 1, 1, 0, NH)
-        quantize_result(1, 0)
         quantize_result(1, 1)
-        store_codes(1, 0, N)
+        store_codes(1, NH, N)
+        quantize_result(1, 0)
+        store_codes(1, 0, NH)
         store_scales(nc.scalar)

from contextlib import ExitStack

import concourse.mybir as mybir

O, K4, N, T = 512, 2560, 512, 1024
FLOPS = 2 * T * N * (O + K4)

F32 = mybir.dt.float32
BF16 = mybir.dt.bfloat16
I32 = mybir.dt.int32
U32 = mybir.dt.uint32
U16 = mybir.dt.uint16
U8 = mybir.dt.uint8
FP8X4 = mybir.dt.float8_e4m3fn_x4
FP4X4 = mybir.dt.float4_e2m1fn_x4

P = 128
PACK = 4
PASSES = K4 // (P * PACK)
HALF = P * PACK
NH = N // 2


def tile_mix_atom_tm_pl_mul_kernel(
    tc, x8, w8, x4_words, x4_scales, w4_words, w4_scales, g, out_0, out_1, out_2
):
    nc = tc.nc
    with ExitStack() as ctx:
        sb = ctx.enter_context(tc.tile_pool(name="sb", bufs=1))
        psum = ctx.enter_context(tc.psum_pool(name="psum", bufs=1))
        ctx.enter_context(tc.manual_schedule())

        def tile(name, shape, dtype):
            return sb.tile(shape, dtype, name=name, align_bytes=64)

        x4_i32 = x4_words.bitcast(I32).rearrange("a p c -> p a c")
        w4_i32 = w4_words.bitcast(I32).rearrange("a p c -> p a c")
        xs_rows = x4_scales.bitcast(I32).rearrange("a (q r) c -> r q a c", r=PACK)
        ws_rows = w4_scales.bitcast(I32).rearrange("a (q r) c -> r q a c", r=PACK)
        os_rows = out_2.bitcast(I32).rearrange("a (q r) c -> r q a c", r=PACK)
        ow_i32 = out_1.rearrange("a p n i -> a p (n i)").bitcast(I32)

        w4_sb = {}
        x4_raw = {}

        def load_w4(a0, a1):
            t = tile("w4_%d" % a0, [P, (a1 - a0) * 2 * N], U8)
            nc.sync.dma_start(
                out=t[:].bitcast(I32).rearrange("p (a c) -> p a c", a=a1 - a0), in_=w4_i32[:, a0:a1, :]
            )
            for a in range(a0, a1):
                w4_sb[a] = t[:, (a - a0) * 2 * N : (a - a0 + 1) * 2 * N]

        def load_x4(a0, a1, h0, h1):
            width = (h1 - h0) * 2 * HALF
            t = tile("x4_%d_%d" % (a0, h0), [P, (a1 - a0) * width], U8)
            nc.sync.dma_start(
                out=t[:].bitcast(I32).rearrange("p (a c) -> p a c", a=a1 - a0),
                in_=x4_i32[:, a0:a1, h0 * HALF // 2 : h1 * HALF // 2],
            )
            for a in range(a0, a1):
                for h in range(h0, h1):
                    c0 = (a - a0) * width + (h - h0) * 2 * HALF
                    x4_raw[h, a] = t[:, c0 : c0 + 2 * HALF]

        def load_scale_rows(plane, rows):
            for r in range(PACK):
                nc.sync.dma_start(
                    out=plane[r:P:32, :].bitcast(I32).rearrange("q (a c) -> q a c", a=PASSES), in_=rows[r]
                )

        def load_rows(name, src):
            t = tile(name, [P, src.shape[1], src.shape[2]], F32)
            nc.sync.dma_start(out=t[:], in_=src)
            return t

        ws_plane = tile("ws_plane", [P, PASSES * N], U8)
        xs_raw = tile("xs_raw", [P, PASSES * T], U8)
        nc.vector.memset(xs_raw[:].bitcast(I32), 0)
        nc.vector.memset(ws_plane[:].bitcast(I32), 0)

        x8_rows = x8.rearrange("(p j) t -> p j t", j=PACK)
        g_rows = g.rearrange("(h p r) n -> h p r n", p=P, r=PACK)
        o_rows = out_0.rearrange("(h p r) n -> h p r n", p=P, r=PACK)

        x8_raw = {}
        g_sb = {}

        def load_x8(h0, h1):
            t = load_rows("x8_raw%d" % h0, x8_rows[:, :, h0 * HALF : h1 * HALF])
            for h in range(h0, h1):
                x8_raw[h] = t[:, :, (h - h0) * HALF : (h - h0 + 1) * HALF]

        def load_g(h, r0, r1):
            t = load_rows("g%d_%d" % (h, r0), g_rows[h, :, r0:r1, :])
            for r in range(r0, r1):
                g_sb[h, r] = t[:, r - r0, :]

        load_w4(0, 1)
        load_x4(0, 1, 0, 2)
        load_scale_rows(xs_raw, xs_rows)
        load_scale_rows(ws_plane, ws_rows)
        load_w4(1, 3)
        load_x4(1, 3, 0, 2)
        load_w4(3, 5)
        load_x4(3, 5, 0, 2)
        w8_raw = load_rows("w8_raw", w8.rearrange("(p j) n -> p j n", j=PACK))
        load_x8(0, 1)
        load_g(0, 0, 2)
        load_x8(1, 2)
        load_g(0, 2, 4)
        load_g(1, 0, 2)
        load_g(1, 2, 4)

        x4_dealt = {}
        xs_dealt = {}

        def deal_words(h, a):
            t = tile("x4d_%d_%d" % (h, a), [P, 2 * HALF], U8)
            nc.scalar.copy(
                out=t[:].bitcast(U16).rearrange("p (r m) -> p r m", r=PACK),
                in_=x4_raw[h, a].bitcast(U16).rearrange("p (m r) -> p r m", r=PACK),
            )
            x4_dealt[h, a] = t

        def deal_scales(h, a0, a1):
            t = tile("xsd_%d_%d" % (h, a0), [P, (a1 - a0) * HALF], U8)
            src = xs_raw[:].rearrange("p (a h m r) -> p h r a m", a=PASSES, h=2, r=PACK)
            nc.vector.tensor_copy(
                out=t[:].rearrange("p (a r m) -> p r a m", r=PACK, m=P), in_=src[:, h, :, a0:a1, :]
            )
            for a in range(a0, a1):
                xs_dealt[h, a] = t[:, (a - a0) * HALF : (a - a0 + 1) * HALF]

        acc = {}
        for h in range(2):
            for r in range(PACK):
                acc[h, r] = psum.tile([P, N], F32, name="acc_%d_%d" % (h, r))
        opened = set()

        def fp4_pass(h, a, rows=range(PACK)):
            for r in rows:
                nc.tensor.matmul_mx(
                    out=acc[h, r][:],
                    lhsT=x4_dealt[h, a][:, 2 * P * r : 2 * P * (r + 1)].bitcast(FP4X4),
                    lhsT_scale=xs_dealt[h, a][:, P * r : P * (r + 1)],
                    rhs=w4_sb[a].bitcast(FP4X4),
                    rhs_scale=ws_plane[:, a * N : (a + 1) * N],
                    start=(h, r) not in opened,
                    stop=False,
                )
                opened.add((h, r))

        w8_codes = tile("w8_codes", [P, N], U32)
        w8_plane = tile("w8_plane", [P, N], U8)
        x8_bf = {}
        x8_codes = {}
        x8_plane = {}

        for h in range(2):
            for rp in range(2):
                x8_bf[h, rp] = tile("x8_bf_%d_%d" % (h, rp), [P, 2 * P * PACK], BF16)

        def round_x8(copy, h, rp, m0=0, m1=P):
            src = x8_raw[h].rearrange("p j (m r) -> p m j r", r=PACK)
            dst = x8_bf[h, rp][:].rearrange("p (r m j) -> p m j r", r=2, j=PACK)
            copy(out=dst[:, m0:m1], in_=src[:, m0:m1, :, 2 * rp : 2 * rp + 2])

        def quantize_x8(h, rp):
            codes = tile("x8_codes_%d_%d" % (h, rp), [P, 2 * P], U32)
            plane = tile("x8_plane_%d_%d" % (h, rp), [P, 2 * P], U8)
            nc.vector.quantize_mx(out=codes[:].bitcast(FP8X4), scales=plane[:], in_=x8_bf[h, rp][:])
            x8_codes[h, rp] = codes
            x8_plane[h, rp] = plane

        def fp8_pass(h, rows=range(PACK)):
            for r in rows:
                cols = slice(P * (r % 2), P * (r % 2 + 1))
                nc.tensor.matmul_mx(
                    out=acc[h, r][:],
                    lhsT=x8_codes[h, r // 2][:, cols].bitcast(FP8X4),
                    lhsT_scale=x8_plane[h, r // 2][:, cols],
                    rhs=w8_codes[:].bitcast(FP8X4),
                    rhs_scale=w8_plane[:],
                    start=False,
                    stop=True,
                )

        res = {h: tile("res_%d" % h, [P, PACK, N], F32) for h in range(2)}
        res_bf = {(h, nh): tile("res_bf_%d_%d" % (h, nh), [P, NH * PACK], BF16) for h in range(2) for nh in range(2)}
        o_codes = {h: tile("o_codes_%d" % h, [P, N], U32) for h in range(2)}
        o_plane = tile("o_plane", [P, 2 * N], U8)

        def gate(h, rows, c0, c1):
            cols = slice(c0, c1)
            for r in rows:
                nc.vector.tensor_tensor(
                    out=res[h][:, r, cols],
                    in0=acc[h, r][:, cols],
                    in1=g_sb[h, r][:, cols],
                    op=mybir.AluOpType.mult,
                )

        def round_result(copy, h, nh, c0, c1):
            src = res[h][:, :, nh * NH + c0 : nh * NH + c1]
            dst = res_bf[h, nh][:, PACK * c0 : PACK * c1]
            copy(
                out=dst.rearrange("p (c i r) -> p c r i", i=4, r=PACK),
                in_=src.rearrange("p r (c i) -> p c r i", i=4),
            )

        def quantize_result(h, nh):
            nc.vector.quantize_mx(
                out=o_codes[h][:, nh * NH : (nh + 1) * NH].bitcast(FP8X4),
                scales=o_plane[:, h * N + nh * NH : h * N + (nh + 1) * NH],
                in_=res_bf[h, nh][:],
            )

        def store_codes(h, c0, c1):
            nc.sync.dma_start(out=ow_i32[h, :, c0:c1], in_=o_codes[h][:, c0:c1].bitcast(I32))

        def store_rows(h, r0, r1):
            nc.sync.dma_start(out=o_rows[h, :, r0:r1, :], in_=res[h][:, r0:r1, :])

        def store_scales(queue, h0=0, h1=2):
            for r in range(PACK):
                queue.dma_start(
                    out=os_rows[r, :, h0:h1, :],
                    in_=o_plane[r:P:32, h0 * N : h1 * N].bitcast(I32).rearrange("q (a c) -> q a c", a=h1 - h0),
                )

        w8_bf = tile("w8_bf", [P, N * PACK], BF16)

        def round_w8(copy, c0, c1):
            copy(
                out=w8_bf[:, PACK * c0 : PACK * c1].rearrange("p (c i j) -> p c j i", i=4, j=PACK),
                in_=w8_raw[:, :, c0:c1].rearrange("p j (c i) -> p c j i", i=4),
            )

        def quantize_w8():
            nc.vector.quantize_mx(out=w8_codes[:].bitcast(FP8X4), scales=w8_plane[:], in_=w8_bf[:])

        V = nc.vector.tensor_copy
        S = nc.scalar.copy

        deal_words(0, 0)
        deal_scales(0, 0, 1)
        fp4_pass(0, 0)
        deal_words(1, 0)
        deal_scales(1, 0, 1)
        fp4_pass(1, 0)
        deal_scales(0, 1, PASSES)
        for a in range(1, PASSES):
            deal_words(0, a)
            fp4_pass(0, a)
        deal_scales(1, 1, PASSES)
        for a in range(1, PASSES):
            deal_words(1, a)
        round_w8(V, 0, N)
        quantize_w8()
        round_x8(V, 0, 0)
        round_x8(S, 0, 1)
        quantize_x8(0, 0)
        quantize_x8(0, 1)
        for a in range(1, 2):
            fp4_pass(1, a)
        fp8_pass(0)
        for a in range(2, 4):
            fp4_pass(1, a)
        fp4_pass(1, 4, range(2))

        gate(0, range(2), 0, N)
        store_rows(0, 0, 2)
        round_x8(V, 1, 0)
        round_x8(S, 1, 1)
        quantize_x8(1, 0)
        fp8_pass(1, range(2))
        fp4_pass(1, 4, range(2, PACK))
        gate(0, range(2, PACK), 0, NH)
        round_result(S, 0, 0, 0, NH)
        quantize_x8(1, 1)
        fp8_pass(1, range(2, PACK))
        gate(0, range(2, PACK), NH, N)
        store_rows(0, 2, 4)
        round_result(S, 0, 1, 0, NH)
        gate(1, range(2), 0, N)
        store_rows(1, 0, 2)
        gate(1, range(2, PACK), 0, NH)
        round_result(S, 1, 0, 0, NH)
        gate(1, range(2, PACK), NH, N)
        store_rows(1, 2, 4)
        quantize_result(0, 0)
        quantize_result(0, 1)
        store_codes(0, 0, N)
        round_result(V, 1, 1, 0, NH)
        quantize_result(1, 1)
        store_codes(1, NH, N)
        quantize_result(1, 0)
        store_codes(1, 0, NH)
        store_scales(nc.scalar)
